import numpy as np
import ml_dtypes


def mxq(x, axis, fmt="e4m3"):
    dtype, down = {"e4m3": (ml_dtypes.float8_e4m3fn, 7), "e5m2": (ml_dtypes.float8_e5m2, 14)}[fmt]
    v = np.moveaxis(np.asarray(x, np.float32).astype(ml_dtypes.bfloat16).astype(np.float64), axis, -1)
    blocks = v.reshape(v.shape[:-1] + (-1, 32))
    amax = np.abs(blocks).max(-1, keepdims=True)
    byte = np.maximum(np.where(amax > 0, np.frexp(amax)[1] - 1 + 127, 0) - down, 1)
    scale = np.exp2(byte - 127.0)
    codes = (blocks / scale).astype(np.float32).astype(dtype).astype(np.float64)
    return np.moveaxis((codes * scale).reshape(v.shape), -1, axis)


WIDE = False


def mx_kscale(k):
    if not WIDE:
        return np.ones(k)
    levels = np.array([10, -10, 5, -5, 0])
    if k % 512:
        return np.exp2(np.random.permutation(np.resize(levels, k // 32))).repeat(32)
    a = np.empty((k // 512, 16))
    for p in range(k // 512):
        a[p, :8] = np.random.permutation(np.resize(levels, 8))
        for g in range(8):
            far = levels[np.abs(levels - a[p, g]) >= 10]
            a[p, g + 8] = far[np.random.randint(len(far))]
    return np.exp2(a.ravel()).repeat(32)


def f64(x):
    return np.asarray(x).astype(np.float64)


def striped(idx):
    return np.tile(idx.reshape(-1, 16).T, (8, 1)).astype(np.uint16)


def unstriped(offs):
    return offs[:16].T.reshape(-1).astype(np.int64)


E2M1 = np.array([0.0, 0.5, 1.0, 1.5, 2.0, 3.0, 4.0, 6.0, -0.0, -0.5, -1.0, -1.5, -2.0, -3.0, -4.0, -6.0])


def pack_weight(w, fmt):
    k, n = w.shape
    w = f64(np.asarray(w, np.float32).astype(ml_dtypes.bfloat16)).reshape(k // 32, 32, n)
    amax = np.abs(w).max(1)
    if fmt == "e4m3":
        byte = np.frexp(amax)[1] - 1 + 127 - 7
    else:
        mant, ex = np.frexp(amax / 6.0)
        byte = np.where(mant > 0.5, ex, ex - 1) + 127
    byte = np.clip(np.where(amax > 0, byte, 1), 1, 254)
    scaled = (w * np.exp2(127.0 - byte)[:, None, :]).reshape(k, n).astype(np.float32)
    by_word = np.ascontiguousarray(scaled.reshape(k // 512, 128, 4, n).transpose(0, 1, 3, 2))
    if fmt == "e4m3":
        words = by_word.astype(ml_dtypes.float8_e4m3fn).view(np.uint8)
    else:
        c = by_word.astype(ml_dtypes.float4_e2m1fn).view(np.uint8) & 0xF
        words = (c[..., 0::2] | (c[..., 1::2] << 4)).reshape(k // 512, 128, 2 * n)
    return np.ascontiguousarray(words), np.ascontiguousarray(byte.astype(np.uint8).reshape(k // 512, 16, n))


def unpack_weight(words, scales, fmt):
    g, _, n = scales.shape
    words = np.ascontiguousarray(words).reshape(g, 128, n, -1)
    if fmt == "e4m3":
        vals = words.view(ml_dtypes.float8_e4m3fn).astype(np.float64)
    else:
        nib = np.empty((g, 128, n, 4), np.uint8)
        nib[..., 0::2] = words & 0xF
        nib[..., 1::2] = words >> 4
        vals = E2M1[nib]
    vals = vals * np.repeat(np.exp2(scales.astype(np.float64) - 127.0), 8, axis=1)[..., None]
    return vals.transpose(0, 1, 3, 2).reshape(g * 512, n)


def gelu(v):
    return 0.5 * v * (1.0 + np.tanh(np.sqrt(2.0 / np.pi) * (v + 0.044715 * v**3)))


K, K2, T, S, H, N = 1024, 1536, 4096, 1024, 512, 384

def setup_inputs():
    n = np.random.standard_normal
    s = mx_kscale(K)[:, None]
    s2 = mx_kscale(K2)[:, None]
    u = mx_kscale(H)[:, None]
    d = {}
    d["tab_words"], d["tab_scales"] = pack_weight(n((K, T)) * s, "e4m3")
    d["offs"] = striped(np.random.permutation(T)[:S])
    d["xs_words"], d["xs_scales"] = pack_weight(n((K2, S)) * s2, "e4m3")
    d["w1"] = (n((K, H)) / s * u.T / K ** 0.5).astype(np.float32)
    d["w2_words"], d["w2_scales"] = pack_weight(n((K, H)) / s * u.T / K ** 0.5, "e4m3")
    d["w3_words"], d["w3_scales"] = pack_weight(n((K2, H)) / s2 * u.T / K2 ** 0.5, "e2m1")
    d["b3"] = (0.7 * n(H) * u[:, 0]).astype(np.float32)
    d["w4"] = (1.4 * n((H, N)) / u / H ** 0.5).astype(np.float32)
    d["b4"] = (0.7 * n(N)).astype(np.float32)
    return d

def reference(tab_words, tab_scales, offs, xs_words, xs_scales, w1, w2_words, w2_scales,
              w3_words, w3_scales, b3, w4, b4):
    v = unpack_weight(tab_words, tab_scales, "e4m3")[:, unstriped(offs)]
    xs = unpack_weight(xs_words, xs_scales, "e4m3")
    w2 = unpack_weight(w2_words, w2_scales, "e4m3")
    w3 = unpack_weight(w3_words, w3_scales, "e2m1")
    hi = mxq(f64(w1), 0, "e4m3").T @ v
    lo = w2.T @ v
    x = (w3.T @ xs) + f64(b3)[:, None]
    h = np.minimum(hi, x) - np.maximum(lo, x)
    y = (mxq(f64(w4), 0, "e4m3").T @ mxq(h, 0, "e4m3")) + f64(b4)[:, None]
    return 1.0 / (1.0 + np.exp(-y))

@@ -1,0 +1,247 @@
+from contextlib import ExitStack
+
+import concourse.mybir as mybir
+from concourse.masks import make_identity
+
+K, K2, T, S, H, N = 1024, 1536, 4096, 1024, 512, 384
+FLOPS = 2 * S * (2 * K * H + K2 * H + H * N)
+
+F32 = mybir.dt.float32
+BF16 = mybir.dt.bfloat16
+I32 = mybir.dt.int32
+U32 = mybir.dt.uint32
+U16 = mybir.dt.uint16
+U8 = mybir.dt.uint8
+FP8X4 = mybir.dt.float8_e4m3fn_x4
+FP4X4 = mybir.dt.float4_e2m1fn_x4
+ALU = mybir.AluOpType
+ACT = mybir.ActivationFunctionType
+
+P = 128
+PA, PB = K // 512, K2 // 512
+HALF, QUART = 512, 256
+NQ = S // QUART
+NT = N // P
+
+
+def tile_list_pasta_crack_scores_kernel(tc, tab_words, tab_scales, offs, xs_words, xs_scales, w1,
+                                                  w2_words, w2_scales, w3_words, w3_scales, b3, w4, b4, out):
+    nc = tc.nc
+    with ExitStack() as ctx:
+        keep = ctx.enter_context(tc.tile_pool(name="keep", bufs=1))
+        ring = ctx.enter_context(tc.tile_pool(name="ring", bufs=3))
+        acc = ctx.enter_context(tc.psum_pool(name="acc", bufs=5))
+        ysum = ctx.enter_context(tc.psum_pool(name="ysum", bufs=3))
+
+        def held(name, shape, dtype):
+            return keep.tile(shape, dtype, name=name, align_bytes=64)
+
+        offsets = held("offsets", [P, S // 16], U16)
+        w3_raw = held("w3_raw", [P, PB, H // 2], I32)
+        xs = [held("xs%d" % c, [P, PB, HALF], I32) for c in range(2)]
+        tab = [held("tab%d" % a, [P, T], I32) for a in range(PA)]
+        w2_raw = held("w2_raw", [P, PA, H], I32)
+        w1_raw = [held("w1_raw%d" % a, [P, 4, H], F32) for a in range(PA)]
+        w4_raw = held("w4_raw", [P, 4, N], F32)
+        w3s_raw = held("w3s_raw", [P, PB, H // 4], I32)
+        w3s = held("w3s", [P, PB * H // 4], I32)
+        xss_raw = held("xss_raw", [P, PB, S // 4], I32)
+        xss = held("xss", [P, PB, S // 4], I32)
+        tabs = keep.tile([P, T // 4], I32, name="tabs", tag="tabs_then_v0", align_bytes=64)
+        w2s_raw = held("w2s_raw", [P, PA, H // 4], I32)
+        w2s = held("w2s", [P, PA * H // 4], I32)
+        bias_raw = held("bias_raw", [P, P], F32)
+        bias_rows = held("bias_rows", [P, P], F32)
+        ident = held("ident", [P, P], F32)
+        bias = held("bias", [P, 8], F32)
+
+        nc.gpsimd.memset(tabs[:], 0)
+        nc.vector.memset(w3s[:], 0)
+        nc.vector.memset(xss[:], 0)
+        nc.vector.memset(bias_rows[:], 0.0)
+        nc.vector.memset(w2s[:], 0)
+        make_identity(nc, ident[:])
+
+        def load_scale_rows(tile, scales):
+            for q in range(4):
+                nc.sync.dma_start(tile[32 * q: 32 * q + 4],
+                                  scales[:, 4 * q: 4 * q + 4, :].rearrange("a r c -> r a c").bitcast(I32))
+
+        xs_src = xs_words.rearrange("a p c i -> p a (c i)")
+        nc.sync.dma_start(w3_raw[:], w3_words.rearrange("a p b -> p a b").bitcast(I32))
+        load_scale_rows(w3s_raw, w3_scales)
+        nc.sync.dma_start(xs[0][:], xs_src[:, :, 0: 4 * HALF].bitcast(I32))
+        load_scale_rows(xss_raw, xs_scales)
+        nc.sync.dma_start(bias_raw[0:4, :].rearrange("t (g u) -> t g u", u=8),
+                          b3.rearrange("(g t u) -> t g u", t=4, u=8))
+        nc.sync.dma_start(bias_raw[4:4 + NT, :], b4.rearrange("(c p) -> c p", p=P))
+        nc.sync.dma_start(xs[1][:], xs_src[:, :, 4 * HALF: 8 * HALF].bitcast(I32))
+        nc.sync.dma_start(offsets[:], offs)
+        for q in range(4):
+            nc.sync.dma_start(tabs[32 * q: 32 * q + 8, :], tab_scales[:, 4 * q: 4 * q + 4, :].bitcast(I32))
+        nc.sync.dma_start(tab[0][:], tab_words[0].rearrange("p t i -> p (t i)").bitcast(I32))
+        load_scale_rows(w2s_raw, w2_scales)
+        nc.sync.dma_start(tab[1][:], tab_words[1].rearrange("p t i -> p (t i)").bitcast(I32))
+        nc.sync.dma_start(w2_raw[:], w2_words.rearrange("a p c i -> p a (c i)").bitcast(I32))
+        for a in range(PA):
+            nc.sync.dma_start(w1_raw[a][:], w1[512 * a: 512 * (a + 1), :].rearrange("(p i) c -> p i c", i=4))
+        w4_src = w4.rearrange("(g t u) n -> t g u n", t=4, u=8)
+        for t in range(4):
+            nc.sync.dma_start(w4_raw[:, t, :], w4_src[t])
+
+        w3p = held("w3p", [P, PB * H // 2], I32)
+        nc.vector.tensor_copy(w3p[:].rearrange("p (a t g w) -> p a t g w", a=PB, t=4, w=4),
+                              w3_raw[:].rearrange("p a (g t w) -> p a t g w", t=4, w=4))
+        for q in range(4):
+            rows = slice(32 * q, 32 * q + 4)
+            nc.vector.tensor_copy(w3s[rows, :].rearrange("p (a t g w) -> p a t g w", a=PB, t=4, w=2),
+                                  w3s_raw[rows].rearrange("p a (g t w) -> p a t g w", t=4, w=2))
+
+        for q in range(4):
+            rows = slice(32 * q, 32 * q + 4)
+            nc.vector.tensor_copy(xss[rows], xss_raw[rows])
+        nc.vector.tensor_copy(bias_rows[0:4 + NT, :], bias_raw[0:4 + NT, :])
+
+        bias_ps = ysum.tile([P, P], F32, name="y")
+        nc.tensor.transpose(bias_ps[:], bias_rows[:], ident[:])
+        nc.scalar.copy(bias[:], bias_ps[:, 0:8])
+
+        xb = [[held("xb%d%d" % (c, u), [P, 2, HALF], F32) for u in range(2)] for c in range(2)]
+        for c in range(2):
+            for t in range(4):
+                bank = acc.tile([P, HALF], F32, name="bank")
+                for a in range(PB):
+                    w0 = (a * 4 + t) * 64
+                    s0 = (a * 4 + t) * 32
+                    nc.tensor.matmul_mx(bank[:], lhsT=w3p[:, w0: w0 + 64].bitcast(FP4X4),
+                                        lhsT_scale=w3s[:, s0: s0 + 32].bitcast(U8),
+                                        rhs=xs[c][:, a, :].bitcast(FP8X4),
+                                        rhs_scale=xss[:, a, 128 * c: 128 * (c + 1)].bitcast(U8),
+                                        start=(a == 0), stop=(a == PB - 1))
+                nc.scalar.activation(xb[c][t // 2][:, t % 2, :], bank[:], ACT.Identity, bias=bias[:, t: t + 1])
+
+        vs = held("vs", [P, S], U8)
+        nc.vector.tensor_copy(vs[:], tabs[:].bitcast(U8).indirect(offsets[:]))
+        v0 = keep.tile([P, S], U32, name="v0", tag="tabs_then_v0", align_bytes=64)
+        nc.vector.tensor_copy(v0[:], tab[0][:].bitcast(U32).indirect(offsets[:]))
+        for q in range(4):
+            rows = slice(32 * q, 32 * q + 4)
+            nc.vector.tensor_copy(w2s[rows, :].rearrange("p (a t g w) -> p a t g w", a=PA, t=4, w=2),
+                                  w2s_raw[rows].rearrange("p a (g t w) -> p a t g w", t=4, w=2))
+        v1 = [held("v1%d" % c, [P, HALF], U32) for c in range(2)]
+        nc.vector.tensor_copy(v1[0][:], tab[1][:].bitcast(U32).indirect(offsets[:, 0:32]))
+        w2p = held("w2p", [P, PA * H], I32)
+        nc.vector.tensor_copy(w2p[:].rearrange("p (a t g w) -> p a t g w", a=PA, t=4, w=8),
+                              w2_raw[:].rearrange("p a (g t w) -> p a t g w", t=4, w=8))
+        nc.vector.tensor_copy(v1[1][:], tab[1][:].bitcast(U32).indirect(offsets[:, 32:64]))
+
+        def table_product(q, u, codes, scales):
+            bank = acc.tile([P, 2, QUART], F32, name="bank")
+            j0 = q * QUART
+            for e in range(2):
+                for a in range(PA):
+                    moving = v0[:, j0: j0 + QUART] if a == 0 else v1[q // 2][:, j0 % HALF: j0 % HALF + QUART]
+                    nc.tensor.matmul_mx(bank[:, e, :], lhsT=codes(a, u, e).bitcast(FP8X4),
+                                        lhsT_scale=scales(a, u, e), rhs=moving.bitcast(FP8X4),
+                                        rhs_scale=vs[4 * a: P, j0: j0 + QUART],
+                                        start=(a == 0), stop=(a == PA - 1))
+            return bank[:].rearrange("p e j -> p j e")
+
+        def x_pair(q, u):
+            j0 = (q % 2) * QUART
+            return xb[q // 2][u][:, :, j0: j0 + QUART].rearrange("p e j -> p j e")
+
+        def w2_codes(a, u, e):
+            c0 = (a * 4 + 2 * u + e) * P
+            return w2p[:, c0: c0 + P]
+
+        def w2_plane(a, u, e):
+            c0 = (a * 4 + 2 * u + e) * 32
+            return w2s[:, c0: c0 + 32].bitcast(U8)
+
+        w1b = [[held("w1b%d%d" % (a, u), [P, 4 * QUART], BF16) for u in range(2)] for a in range(PA)]
+        w1c = [[held("w1c%d%d" % (a, u), [P, QUART], U32) for u in range(2)] for a in range(PA)]
+        w1s = [[held("w1s%d%d" % (a, u), [P, QUART], U8) for u in range(2)] for a in range(PA)]
+
+        def round_w1(a, u):
+            src = w1_raw[a][:].rearrange("p i (g t w) -> p t g w i", t=4, w=8)
+            nc.scalar.copy(w1b[a][u][:].rearrange("p (e g w i) -> p e g w i", e=2, w=8, i=4),
+                           src[:, 2 * u: 2 * u + 2])
+
+        def quantise_w1(a, u):
+            nc.vector.quantize_mx(w1c[a][u][:].bitcast(FP8X4), w1s[a][u][:], w1b[a][u][:])
+
+        floor = [held("floor%d" % q, [P, 2, QUART, 2], F32) for q in range(NQ)]
+        w1_pieces = [(a, u) for a in range(PA) for u in range(2)]
+        for a, u in w1_pieces:
+            round_w1(a, u)
+        for q in range(NQ):
+            for u in range(2):
+                lo = table_product(q, u, w2_codes, w2_plane)
+                nc.vector.tensor_tensor(floor[q][:, u], lo, x_pair(q, u), ALU.max)
+            if q >= 1:
+                quantise_w1(*w1_pieces[q - 1])
+        quantise_w1(*w1_pieces[NQ - 1])
+
+        w4b = held("w4b", [P, N, 4], BF16)
+        nc.scalar.copy(w4b[:], w4_raw[:].rearrange("p t n -> p n t"))
+        w4c = held("w4c", [P, N], U32)
+        w4s = held("w4s", [P, N], U8)
+        w4_flat = w4b[:].rearrange("p n t -> p (n t)")
+
+        def w1_codes(a, u, e):
+            return w1c[a][u][:, e * P: (e + 1) * P]
+
+        def w1_plane(a, u, e):
+            return w1s[a][u][:, e * P: (e + 1) * P]
+
+        ceil = {}
+        hb = {}
+
+        def upper(q, u):
+            if u == 0:
+                ceil[q] = ring.tile([P, 2, QUART, 2], F32, name="ceil")
+            hi = table_product(q, u, w1_codes, w1_plane)
+            nc.vector.tensor_tensor(ceil[q][:, u], hi, x_pair(q, u), ALU.min)
+
+        def difference(q, j0, n):
+            hb[q, j0] = ring.tile([P, n, 2, 2], BF16, name="hb", align_bytes=64)
+            nc.vector.tensor_tensor(hb[q, j0][:], ceil[q][:, :, j0: j0 + n].rearrange("p u j e -> p j u e"),
+                                    floor[q][:, :, j0: j0 + n].rearrange("p u j e -> p j u e"), ALU.subtract)
+
+        out_v = out.rearrange("(c p) j -> p c j", p=P)
+
+        def scores(q, j0, n):
+            hc = ring.tile([P, n], U32, name="hc", align_bytes=64)
+            hs = ring.tile([P, n], U8, name="hs", align_bytes=64)
+            nc.vector.quantize_mx(hc[:].bitcast(FP8X4), hs[:], hb[q, j0][:].rearrange("p j u e -> p (j u e)"))
+            res = ring.tile([P, NT, n], F32, name="res")
+            for c in range(NT):
+                y = ysum.tile([P, n], F32, name="y")
+                nc.tensor.matmul_mx(y[:], lhsT=w4c[:, c * P: (c + 1) * P].bitcast(FP8X4),
+                                    lhsT_scale=w4s[:, c * P: (c + 1) * P], rhs=hc[:].bitcast(FP8X4),
+                                    rhs_scale=hs[:], start=True, stop=True)
+                nc.scalar.activation(res[:, c, :], y[:], ACT.Sigmoid, bias=bias[:, 4 + c: 5 + c])
+            col = q * QUART + j0
+            nc.sync.dma_start(out_v[:, :, col: col + n], res[:])
+
+        upper(0, 0)
+        upper(1, 0)
+        upper(0, 1)
+        upper(1, 1)
+        difference(0, 0, QUART)
+        nc.vector.quantize_mx(w4c[:, 0:256].bitcast(FP8X4), w4s[:, 0:256], w4_flat[:, 0:1024])
+        nc.vector.quantize_mx(w4c[:, 256:N].bitcast(FP8X4), w4s[:, 256:N], w4_flat[:, 1024:4 * N])
+        scores(0, 0, QUART)
+        difference(1, 0, QUART)
+        upper(2, 0)
+        scores(1, 0, QUART)
+        upper(2, 1)
+        upper(3, 0)
+        difference(2, 0, QUART)
+        upper(3, 1)
+        scores(2, 0, QUART)
+        difference(3, 0, P)
+        difference(3, P, P)
+        scores(3, 0, P)
+        scores(3, P, P)

@@ -22,6 +22,7 @@ PA, PB = K // 512, K2 // 512
 HALF, QUART = 512, 256
 NQ = S // QUART
 NT = N // P
+ROW0 = 8
 
 
 def tile_list_pasta_crack_scores_kernel(tc, tab_words, tab_scales, offs, xs_words, xs_scales, w1,
@@ -39,55 +40,58 @@ def tile_list_pasta_crack_scores_kernel(tc, tab_words, tab_scales, offs, xs_word
         offsets = held("offsets", [P, S // 16], U16)
         w3_raw = held("w3_raw", [P, PB, H // 2], I32)
         xs = [held("xs%d" % c, [P, PB, HALF], I32) for c in range(2)]
-        tab = [held("tab%d" % a, [P, T], I32) for a in range(PA)]
+        tab = [keep.tile([P, T], I32, name="tab%d" % a, tag="tab%d" % a, align_bytes=64) for a in range(PA)]
         w2_raw = held("w2_raw", [P, PA, H], I32)
         w1_raw = [held("w1_raw%d" % a, [P, 4, H], F32) for a in range(PA)]
         w4_raw = held("w4_raw", [P, 4, N], F32)
         w3s_raw = held("w3s_raw", [P, PB, H // 4], I32)
         w3s = held("w3s", [P, PB * H // 4], I32)
-        xss_raw = held("xss_raw", [P, PB, S // 4], I32)
+        xss_raw = keep.tile([P, PB, S // 4], I32, name="xss_raw", tag="xss_then_vs", align_bytes=64)
         xss = held("xss", [P, PB, S // 4], I32)
-        tabs = keep.tile([P, T // 4], I32, name="tabs", tag="tabs_then_v0", align_bytes=64)
-        w2s_raw = held("w2s_raw", [P, PA, H // 4], I32)
-        w2s = held("w2s", [P, PA * H // 4], I32)
+        tabs = keep.tile([P, T // 4], I32, name="tabs", tag="tabs_then_w2s", align_bytes=64)
+        w2s_raw = keep.tile([P, H // 4], I32, name="w2s_raw", tag="w2s_then_v0", align_bytes=64)
         bias_raw = held("bias_raw", [P, P], F32)
         bias_rows = held("bias_rows", [P, P], F32)
         ident = held("ident", [P, P], F32)
         bias = held("bias", [P, 8], F32)
 
+        make_identity(nc, ident[:])
         nc.gpsimd.memset(tabs[:], 0)
+        nc.vector.memset(w2s_raw[:], 0)
         nc.vector.memset(w3s[:], 0)
         nc.vector.memset(xss[:], 0)
         nc.vector.memset(bias_rows[:], 0.0)
-        nc.vector.memset(w2s[:], 0)
-        make_identity(nc, ident[:])
 
         def load_scale_rows(tile, scales):
             for q in range(4):
                 nc.sync.dma_start(tile[32 * q: 32 * q + 4],
                                   scales[:, 4 * q: 4 * q + 4, :].rearrange("a r c -> r a c").bitcast(I32))
 
+        def load_packed_rows(tile, scales):
+            for q in range(4):
+                nc.gpsimd.dma_start(tile[32 * q + ROW0: 32 * q + ROW0 + 8, :],
+                                    scales[:, 4 * q: 4 * q + 4, :].bitcast(I32))
+
         xs_src = xs_words.rearrange("a p c i -> p a (c i)")
         nc.sync.dma_start(w3_raw[:], w3_words.rearrange("a p b -> p a b").bitcast(I32))
         load_scale_rows(w3s_raw, w3_scales)
         nc.sync.dma_start(xs[0][:], xs_src[:, :, 0: 4 * HALF].bitcast(I32))
+        nc.sync.dma_start(offsets[:], offs)
+        nc.sync.dma_start(xs[1][:], xs_src[:, :, 4 * HALF: 8 * HALF].bitcast(I32))
         load_scale_rows(xss_raw, xs_scales)
         nc.sync.dma_start(bias_raw[0:4, :].rearrange("t (g u) -> t g u", u=8),
                           b3.rearrange("(g t u) -> t g u", t=4, u=8))
         nc.sync.dma_start(bias_raw[4:4 + NT, :], b4.rearrange("(c p) -> c p", p=P))
-        nc.sync.dma_start(xs[1][:], xs_src[:, :, 4 * HALF: 8 * HALF].bitcast(I32))
-        nc.sync.dma_start(offsets[:], offs)
-        for q in range(4):
-            nc.sync.dma_start(tabs[32 * q: 32 * q + 8, :], tab_scales[:, 4 * q: 4 * q + 4, :].bitcast(I32))
-        nc.sync.dma_start(tab[0][:], tab_words[0].rearrange("p t i -> p (t i)").bitcast(I32))
-        load_scale_rows(w2s_raw, w2_scales)
-        nc.sync.dma_start(tab[1][:], tab_words[1].rearrange("p t i -> p (t i)").bitcast(I32))
+        for a in range(PA):
+            nc.sync.dma_start(tab[a][:], tab_words[a].rearrange("p t i -> p (t i)").bitcast(I32))
         nc.sync.dma_start(w2_raw[:], w2_words.rearrange("a p c i -> p a (c i)").bitcast(I32))
         for a in range(PA):
             nc.sync.dma_start(w1_raw[a][:], w1[512 * a: 512 * (a + 1), :].rearrange("(p i) c -> p i c", i=4))
         w4_src = w4.rearrange("(g t u) n -> t g u n", t=4, u=8)
         for t in range(4):
             nc.sync.dma_start(w4_raw[:, t, :], w4_src[t])
+        load_packed_rows(tabs, tab_scales)
+        load_packed_rows(w2s_raw, w2_scales)
 
         w3p = held("w3p", [P, PB * H // 2], I32)
         nc.vector.tensor_copy(w3p[:].rearrange("p (a t g w) -> p a t g w", a=PB, t=4, w=4),
@@ -97,16 +101,17 @@ def tile_list_pasta_crack_scores_kernel(tc, tab_words, tab_scales, offs, xs_word
             nc.vector.tensor_copy(w3s[rows, :].rearrange("p (a t g w) -> p a t g w", a=PB, t=4, w=2),
                                   w3s_raw[rows].rearrange("p a (g t w) -> p a t g w", t=4, w=2))
 
+        nc.vector.tensor_copy(bias_rows[0:4 + NT, :], bias_raw[0:4 + NT, :])
         for q in range(4):
             rows = slice(32 * q, 32 * q + 4)
             nc.vector.tensor_copy(xss[rows], xss_raw[rows])
-        nc.vector.tensor_copy(bias_rows[0:4 + NT, :], bias_raw[0:4 + NT, :])
 
         bias_ps = ysum.tile([P, P], F32, name="y")
         nc.tensor.transpose(bias_ps[:], bias_rows[:], ident[:])
         nc.scalar.copy(bias[:], bias_ps[:, 0:8])
 
         xb = [[held("xb%d%d" % (c, u), [P, 2, HALF], F32) for u in range(2)] for c in range(2)]
+        xp = [[held("xp%d%d" % (c, u), [P, HALF, 2], F32) for u in range(2)] for c in range(2)]
         for c in range(2):
             for t in range(4):
                 bank = acc.tile([P, HALF], F32, name="bank")
@@ -119,18 +124,19 @@ def tile_list_pasta_crack_scores_kernel(tc, tab_words, tab_scales, offs, xs_word
                                         rhs_scale=xss[:, a, 128 * c: 128 * (c + 1)].bitcast(U8),
                                         start=(a == 0), stop=(a == PB - 1))
                 nc.scalar.activation(xb[c][t // 2][:, t % 2, :], bank[:], ACT.Identity, bias=bias[:, t: t + 1])
+                if t % 2 == 1:
+                    nc.scalar.copy(xp[c][t // 2][:], xb[c][t // 2][:].rearrange("p e j -> p j e"))
 
-        vs = held("vs", [P, S], U8)
+        vs = keep.tile([P, S], U8, name="vs", tag="xss_then_vs", align_bytes=64)
         nc.vector.tensor_copy(vs[:], tabs[:].bitcast(U8).indirect(offsets[:]))
-        v0 = keep.tile([P, S], U32, name="v0", tag="tabs_then_v0", align_bytes=64)
+        w2s = keep.tile([P, H // 4], I32, name="w2s", tag="tabs_then_w2s", align_bytes=64)
+        nc.vector.tensor_copy(w2s[:].rearrange("p (t g w) -> p t g w", t=4, w=2),
+                              w2s_raw[:].rearrange("p (g t w) -> p t g w", t=4, w=2))
+        v0 = keep.tile([P, S], U32, name="v0", tag="w2s_then_v0", align_bytes=64)
         nc.vector.tensor_copy(v0[:], tab[0][:].bitcast(U32).indirect(offsets[:]))
-        for q in range(4):
-            rows = slice(32 * q, 32 * q + 4)
-            nc.vector.tensor_copy(w2s[rows, :].rearrange("p (a t g w) -> p a t g w", a=PA, t=4, w=2),
-                                  w2s_raw[rows].rearrange("p a (g t w) -> p a t g w", t=4, w=2))
         v1 = [held("v1%d" % c, [P, HALF], U32) for c in range(2)]
         nc.vector.tensor_copy(v1[0][:], tab[1][:].bitcast(U32).indirect(offsets[:, 0:32]))
-        w2p = held("w2p", [P, PA * H], I32)
+        w2p = keep.tile([P, PA * H], I32, name="w2p", tag="tab0", align_bytes=64)
         nc.vector.tensor_copy(w2p[:].rearrange("p (a t g w) -> p a t g w", a=PA, t=4, w=8),
                               w2_raw[:].rearrange("p a (g t w) -> p a t g w", t=4, w=8))
         nc.vector.tensor_copy(v1[1][:], tab[1][:].bitcast(U32).indirect(offsets[:, 32:64]))
@@ -143,30 +149,31 @@ def tile_list_pasta_crack_scores_kernel(tc, tab_words, tab_scales, offs, xs_word
                     moving = v0[:, j0: j0 + QUART] if a == 0 else v1[q // 2][:, j0 % HALF: j0 % HALF + QUART]
                     nc.tensor.matmul_mx(bank[:, e, :], lhsT=codes(a, u, e).bitcast(FP8X4),
                                         lhsT_scale=scales(a, u, e), rhs=moving.bitcast(FP8X4),
-                                        rhs_scale=vs[4 * a: P, j0: j0 + QUART],
+                                        rhs_scale=vs[ROW0 + 4 * a: P, j0: j0 + QUART],
                                         start=(a == 0), stop=(a == PA - 1))
             return bank[:].rearrange("p e j -> p j e")
 
         def x_pair(q, u):
             j0 = (q % 2) * QUART
-            return xb[q // 2][u][:, :, j0: j0 + QUART].rearrange("p e j -> p j e")
+            return xp[q // 2][u][:, j0: j0 + QUART, :]
 
         def w2_codes(a, u, e):
             c0 = (a * 4 + 2 * u + e) * P
             return w2p[:, c0: c0 + P]
 
         def w2_plane(a, u, e):
-            c0 = (a * 4 + 2 * u + e) * 32
-            return w2s[:, c0: c0 + 32].bitcast(U8)
+            c0 = (2 * u + e) * 32
+            return w2s[ROW0 + 4 * a: P, c0: c0 + 32].bitcast(U8)
 
         w1b = [[held("w1b%d%d" % (a, u), [P, 4 * QUART], BF16) for u in range(2)] for a in range(PA)]
         w1c = [[held("w1c%d%d" % (a, u), [P, QUART], U32) for u in range(2)] for a in range(PA)]
         w1s = [[held("w1s%d%d" % (a, u), [P, QUART], U8) for u in range(2)] for a in range(PA)]
 
         def round_w1(a, u):
-            src = w1_raw[a][:].rearrange("p i (g t w) -> p t g w i", t=4, w=8)
-            nc.scalar.copy(w1b[a][u][:].rearrange("p (e g w i) -> p e g w i", e=2, w=8, i=4),
-                           src[:, 2 * u: 2 * u + 2])
+            src = w1_raw[a][:].rearrange("p i (g t h w) -> p t g h i w", t=4, h=2, w=4)
+            dst = w1b[a][u][:].rearrange("p (e g h w i) -> p e g h i w", e=2, h=2, w=4, i=4)
+            for e in range(2):
+                nc.scalar.copy(dst[:, e], src[:, 2 * u + e])
 
         def quantise_w1(a, u):
             nc.vector.quantize_mx(w1c[a][u][:].bitcast(FP8X4), w1s[a][u][:], w1b[a][u][:])
@@ -184,7 +191,7 @@ def tile_list_pasta_crack_scores_kernel(tc, tab_words, tab_scales, offs, xs_word
         quantise_w1(*w1_pieces[NQ - 1])
 
         w4b = held("w4b", [P, N, 4], BF16)
-        nc.scalar.copy(w4b[:], w4_raw[:].rearrange("p t n -> p n t"))
+        nc.scalar.copy(w4b[:].rearrange("p (m w) t -> p m t w", w=4), w4_raw[:].rearrange("p t (m w) -> p m t w", w=4))
         w4c = held("w4c", [P, N], U32)
         w4s = held("w4s", [P, N], U8)
         w4_flat = w4b[:].rearrange("p n t -> p (n t)")
@@ -235,10 +242,10 @@ def tile_list_pasta_crack_scores_kernel(tc, tab_words, tab_scales, offs, xs_word
         scores(0, 0, QUART)
         difference(1, 0, QUART)
         upper(2, 0)
-        scores(1, 0, QUART)
         upper(2, 1)
-        upper(3, 0)
+        scores(1, 0, QUART)
         difference(2, 0, QUART)
+        upper(3, 0)
         upper(3, 1)
         scores(2, 0, QUART)
         difference(3, 0, P)

@@ -47,52 +47,54 @@ def tile_list_pasta_crack_scores_kernel(tc, tab_words, tab_scales, offs, xs_word
         w3s_raw = held("w3s_raw", [P, PB, H // 4], I32)
         w3s = held("w3s", [P, PB * H // 4], I32)
         xss_raw = keep.tile([P, PB, S // 4], I32, name="xss_raw", tag="xss_then_vs", align_bytes=64)
-        xss = held("xss", [P, PB, S // 4], I32)
-        tabs = keep.tile([P, T // 4], I32, name="tabs", tag="tabs_then_w2s", align_bytes=64)
-        w2s_raw = keep.tile([P, H // 4], I32, name="w2s_raw", tag="w2s_then_v0", align_bytes=64)
+        xss = [held("xss%d" % c, [P, PB, HALF // 4], I32) for c in range(2)]
+        tabs = keep.tile([P, T // 4], I32, name="tabs", tag="tabs_then_v0", align_bytes=64)
+        w2s_raw = held("w2s_raw", [P, H // 4], I32)
         bias_raw = held("bias_raw", [P, P], F32)
         bias_rows = held("bias_rows", [P, P], F32)
         ident = held("ident", [P, P], F32)
         bias = held("bias", [P, 8], F32)
 
         make_identity(nc, ident[:])
-        nc.gpsimd.memset(tabs[:], 0)
+        nc.vector.memset(tabs[:], 0)
         nc.vector.memset(w2s_raw[:], 0)
-        nc.vector.memset(w3s[:], 0)
-        nc.vector.memset(xss[:], 0)
         nc.vector.memset(bias_rows[:], 0.0)
+        nc.vector.memset(w3s[:], 0)
+        for c in range(2):
+            nc.vector.memset(xss[c][:], 0)
 
         def load_scale_rows(tile, scales):
             for q in range(4):
                 nc.sync.dma_start(tile[32 * q: 32 * q + 4],
                                   scales[:, 4 * q: 4 * q + 4, :].rearrange("a r c -> r a c").bitcast(I32))
 
-        def load_packed_rows(tile, scales):
+        def load_packed_rows(queue, tile, scales):
             for q in range(4):
-                nc.gpsimd.dma_start(tile[32 * q + ROW0: 32 * q + ROW0 + 8, :],
+                queue.dma_start(tile[32 * q + ROW0: 32 * q + ROW0 + 8, :],
                                     scales[:, 4 * q: 4 * q + 4, :].bitcast(I32))
 
         xs_src = xs_words.rearrange("a p c i -> p a (c i)")
+        nc.scalar.dma_start(bias_raw[0:4, :].rearrange("t (g u) -> t g u", u=8),
+                            b3.rearrange("(g t u) -> t g u", t=4, u=8))
+        nc.scalar.dma_start(bias_raw[4:4 + NT, :], b4.rearrange("(c p) -> c p", p=P))
         nc.sync.dma_start(w3_raw[:], w3_words.rearrange("a p b -> p a b").bitcast(I32))
         load_scale_rows(w3s_raw, w3_scales)
         nc.sync.dma_start(xs[0][:], xs_src[:, :, 0: 4 * HALF].bitcast(I32))
+        load_scale_rows(xss_raw, xs_scales)
         nc.sync.dma_start(offsets[:], offs)
         nc.sync.dma_start(xs[1][:], xs_src[:, :, 4 * HALF: 8 * HALF].bitcast(I32))
-        load_scale_rows(xss_raw, xs_scales)
-        nc.sync.dma_start(bias_raw[0:4, :].rearrange("t (g u) -> t g u", u=8),
-                          b3.rearrange("(g t u) -> t g u", t=4, u=8))
-        nc.sync.dma_start(bias_raw[4:4 + NT, :], b4.rearrange("(c p) -> c p", p=P))
-        for a in range(PA):
-            nc.sync.dma_start(tab[a][:], tab_words[a].rearrange("p t i -> p (t i)").bitcast(I32))
+        nc.sync.dma_start(tab[0][:], tab_words[0].rearrange("p t i -> p (t i)").bitcast(I32))
+        load_packed_rows(nc.sync, w2s_raw, w2_scales)
+        nc.sync.dma_start(tab[1][:], tab_words[1].rearrange("p t i -> p (t i)").bitcast(I32))
         nc.sync.dma_start(w2_raw[:], w2_words.rearrange("a p c i -> p a (c i)").bitcast(I32))
         for a in range(PA):
             nc.sync.dma_start(w1_raw[a][:], w1[512 * a: 512 * (a + 1), :].rearrange("(p i) c -> p i c", i=4))
         w4_src = w4.rearrange("(g t u) n -> t g u n", t=4, u=8)
         for t in range(4):
             nc.sync.dma_start(w4_raw[:, t, :], w4_src[t])
-        load_packed_rows(tabs, tab_scales)
-        load_packed_rows(w2s_raw, w2_scales)
+        load_packed_rows(nc.gpsimd, tabs, tab_scales)
 
+        nc.vector.tensor_copy(bias_rows[0:4 + NT, :], bias_raw[0:4 + NT, :])
         w3p = held("w3p", [P, PB * H // 2], I32)
         nc.vector.tensor_copy(w3p[:].rearrange("p (a t g w) -> p a t g w", a=PB, t=4, w=4),
                               w3_raw[:].rearrange("p a (g t w) -> p a t g w", t=4, w=4))
@@ -101,10 +103,10 @@ def tile_list_pasta_crack_scores_kernel(tc, tab_words, tab_scales, offs, xs_word
             nc.vector.tensor_copy(w3s[rows, :].rearrange("p (a t g w) -> p a t g w", a=PB, t=4, w=2),
                                   w3s_raw[rows].rearrange("p a (g t w) -> p a t g w", t=4, w=2))
 
-        nc.vector.tensor_copy(bias_rows[0:4 + NT, :], bias_raw[0:4 + NT, :])
-        for q in range(4):
-            rows = slice(32 * q, 32 * q + 4)
-            nc.vector.tensor_copy(xss[rows], xss_raw[rows])
+        for c in range(2):
+            for q in range(4):
+                rows = slice(32 * q, 32 * q + 4)
+                nc.vector.tensor_copy(xss[c][rows], xss_raw[rows, :, P * c: P * (c + 1)])
 
         bias_ps = ysum.tile([P, P], F32, name="y")
         nc.tensor.transpose(bias_ps[:], bias_rows[:], ident[:])
@@ -121,7 +123,7 @@ def tile_list_pasta_crack_scores_kernel(tc, tab_words, tab_scales, offs, xs_word
                     nc.tensor.matmul_mx(bank[:], lhsT=w3p[:, w0: w0 + 64].bitcast(FP4X4),
                                         lhsT_scale=w3s[:, s0: s0 + 32].bitcast(U8),
                                         rhs=xs[c][:, a, :].bitcast(FP8X4),
-                                        rhs_scale=xss[:, a, 128 * c: 128 * (c + 1)].bitcast(U8),
+                                        rhs_scale=xss[c][:, a, :].bitcast(U8),
                                         start=(a == 0), stop=(a == PB - 1))
                 nc.scalar.activation(xb[c][t // 2][:, t % 2, :], bank[:], ACT.Identity, bias=bias[:, t: t + 1])
                 if t % 2 == 1:
@@ -129,11 +131,11 @@ def tile_list_pasta_crack_scores_kernel(tc, tab_words, tab_scales, offs, xs_word
 
         vs = keep.tile([P, S], U8, name="vs", tag="xss_then_vs", align_bytes=64)
         nc.vector.tensor_copy(vs[:], tabs[:].bitcast(U8).indirect(offsets[:]))
-        w2s = keep.tile([P, H // 4], I32, name="w2s", tag="tabs_then_w2s", align_bytes=64)
+        v0 = keep.tile([P, S], U32, name="v0", tag="tabs_then_v0", align_bytes=64)
+        nc.vector.tensor_copy(v0[:], tab[0][:].bitcast(U32).indirect(offsets[:]))
+        w2s = held("w2s", [P, H // 4], I32)
         nc.vector.tensor_copy(w2s[:].rearrange("p (t g w) -> p t g w", t=4, w=2),
                               w2s_raw[:].rearrange("p (g t w) -> p t g w", t=4, w=2))
-        v0 = keep.tile([P, S], U32, name="v0", tag="w2s_then_v0", align_bytes=64)
-        nc.vector.tensor_copy(v0[:], tab[0][:].bitcast(U32).indirect(offsets[:]))
         v1 = [held("v1%d" % c, [P, HALF], U32) for c in range(2)]
         nc.vector.tensor_copy(v1[0][:], tab[1][:].bitcast(U32).indirect(offsets[:, 0:32]))
         w2p = keep.tile([P, PA * H], I32, name="w2p", tag="tab0", align_bytes=64)
@@ -230,7 +232,8 @@ def tile_list_pasta_crack_scores_kernel(tc, tab_words, tab_scales, offs, xs_word
                                     rhs_scale=hs[:], start=True, stop=True)
                 nc.scalar.activation(res[:, c, :], y[:], ACT.Sigmoid, bias=bias[:, 4 + c: 5 + c])
             col = q * QUART + j0
-            nc.sync.dma_start(out_v[:, :, col: col + n], res[:])
+            queue = nc.scalar if col + n == S else nc.sync
+            queue.dma_start(out_v[:, :, col: col + n], res[:])
 
         upper(0, 0)
         upper(1, 0)
@@ -244,10 +247,12 @@ def tile_list_pasta_crack_scores_kernel(tc, tab_words, tab_scales, offs, xs_word
         upper(2, 0)
         upper(2, 1)
         scores(1, 0, QUART)
-        difference(2, 0, QUART)
+        difference(2, 0, P)
         upper(3, 0)
+        scores(2, 0, P)
+        difference(2, P, P)
         upper(3, 1)
-        scores(2, 0, QUART)
+        scores(2, P, P)
         difference(3, 0, P)
         difference(3, P, P)
         scores(3, 0, P)

from contextlib import ExitStack

import concourse.mybir as mybir
from concourse.masks import make_identity

K, K2, T, S, H, N = 1024, 1536, 4096, 1024, 512, 384
FLOPS = 2 * S * (2 * K * H + K2 * H + H * N)

F32 = mybir.dt.float32
BF16 = mybir.dt.bfloat16
I32 = mybir.dt.int32
U32 = mybir.dt.uint32
U16 = mybir.dt.uint16
U8 = mybir.dt.uint8
FP8X4 = mybir.dt.float8_e4m3fn_x4
FP4X4 = mybir.dt.float4_e2m1fn_x4
ALU = mybir.AluOpType
ACT = mybir.ActivationFunctionType

P = 128
PA, PB = K // 512, K2 // 512
HALF, QUART = 512, 256
NQ = S // QUART
NT = N // P
ROW0 = 8


def tile_list_pasta_crack_scores_kernel(tc, tab_words, tab_scales, offs, xs_words, xs_scales, w1,
                                                  w2_words, w2_scales, w3_words, w3_scales, b3, w4, b4, out):
    nc = tc.nc
    with ExitStack() as ctx:
        keep = ctx.enter_context(tc.tile_pool(name="keep", bufs=1))
        ring = ctx.enter_context(tc.tile_pool(name="ring", bufs=3))
        acc = ctx.enter_context(tc.psum_pool(name="acc", bufs=5))
        ysum = ctx.enter_context(tc.psum_pool(name="ysum", bufs=3))

        def held(name, shape, dtype):
            return keep.tile(shape, dtype, name=name, align_bytes=64)

        offsets = held("offsets", [P, S // 16], U16)
        w3_raw = held("w3_raw", [P, PB, H // 2], I32)
        xs = [held("xs%d" % c, [P, PB, HALF], I32) for c in range(2)]
        tab = [keep.tile([P, T], I32, name="tab%d" % a, tag="tab%d" % a, align_bytes=64) for a in range(PA)]
        w2_raw = held("w2_raw", [P, PA, H], I32)
        w1_raw = [held("w1_raw%d" % a, [P, 4, H], F32) for a in range(PA)]
        w4_raw = held("w4_raw", [P, 4, N], F32)
        w3s_raw = held("w3s_raw", [P, PB, H // 4], I32)
        w3s = held("w3s", [P, PB * H // 4], I32)
        xss_raw = keep.tile([P, PB, S // 4], I32, name="xss_raw", tag="xss_then_vs", align_bytes=64)
        xss = [held("xss%d" % c, [P, PB, HALF // 4], I32) for c in range(2)]
        tabs = keep.tile([P, T // 4], I32, name="tabs", tag="tabs_then_v0", align_bytes=64)
        w2s_raw = held("w2s_raw", [P, H // 4], I32)
        bias_raw = held("bias_raw", [P, P], F32)
        bias_rows = held("bias_rows", [P, P], F32)
        ident = held("ident", [P, P], F32)
        bias = held("bias", [P, 8], F32)

        make_identity(nc, ident[:])
        nc.vector.memset(tabs[:], 0)
        nc.vector.memset(w2s_raw[:], 0)
        nc.vector.memset(bias_rows[:], 0.0)
        nc.vector.memset(w3s[:], 0)
        for c in range(2):
            nc.vector.memset(xss[c][:], 0)

        def load_scale_rows(tile, scales):
            for q in range(4):
                nc.sync.dma_start(tile[32 * q: 32 * q + 4],
                                  scales[:, 4 * q: 4 * q + 4, :].rearrange("a r c -> r a c").bitcast(I32))

        def load_packed_rows(queue, tile, scales):
            for q in range(4):
                queue.dma_start(tile[32 * q + ROW0: 32 * q + ROW0 + 8, :],
                                    scales[:, 4 * q: 4 * q + 4, :].bitcast(I32))

        xs_src = xs_words.rearrange("a p c i -> p a (c i)")
        nc.scalar.dma_start(bias_raw[0:4, :].rearrange("t (g u) -> t g u", u=8),
                            b3.rearrange("(g t u) -> t g u", t=4, u=8))
        nc.scalar.dma_start(bias_raw[4:4 + NT, :], b4.rearrange("(c p) -> c p", p=P))
        nc.sync.dma_start(w3_raw[:], w3_words.rearrange("a p b -> p a b").bitcast(I32))
        load_scale_rows(w3s_raw, w3_scales)
        nc.sync.dma_start(xs[0][:], xs_src[:, :, 0: 4 * HALF].bitcast(I32))
        load_scale_rows(xss_raw, xs_scales)
        nc.sync.dma_start(offsets[:], offs)
        nc.sync.dma_start(xs[1][:], xs_src[:, :, 4 * HALF: 8 * HALF].bitcast(I32))
        nc.sync.dma_start(tab[0][:], tab_words[0].rearrange("p t i -> p (t i)").bitcast(I32))
        load_packed_rows(nc.sync, w2s_raw, w2_scales)
        nc.sync.dma_start(tab[1][:], tab_words[1].rearrange("p t i -> p (t i)").bitcast(I32))
        nc.sync.dma_start(w2_raw[:], w2_words.rearrange("a p c i -> p a (c i)").bitcast(I32))
        for a in range(PA):
            nc.sync.dma_start(w1_raw[a][:], w1[512 * a: 512 * (a + 1), :].rearrange("(p i) c -> p i c", i=4))
        w4_src = w4.rearrange("(g t u) n -> t g u n", t=4, u=8)
        for t in range(4):
            nc.sync.dma_start(w4_raw[:, t, :], w4_src[t])
        load_packed_rows(nc.gpsimd, tabs, tab_scales)

        nc.vector.tensor_copy(bias_rows[0:4 + NT, :], bias_raw[0:4 + NT, :])
        w3p = held("w3p", [P, PB * H // 2], I32)
        nc.vector.tensor_copy(w3p[:].rearrange("p (a t g w) -> p a t g w", a=PB, t=4, w=4),
                              w3_raw[:].rearrange("p a (g t w) -> p a t g w", t=4, w=4))
        for q in range(4):
            rows = slice(32 * q, 32 * q + 4)
            nc.vector.tensor_copy(w3s[rows, :].rearrange("p (a t g w) -> p a t g w", a=PB, t=4, w=2),
                                  w3s_raw[rows].rearrange("p a (g t w) -> p a t g w", t=4, w=2))

        for c in range(2):
            for q in range(4):
                rows = slice(32 * q, 32 * q + 4)
                nc.vector.tensor_copy(xss[c][rows], xss_raw[rows, :, P * c: P * (c + 1)])

        bias_ps = ysum.tile([P, P], F32, name="y")
        nc.tensor.transpose(bias_ps[:], bias_rows[:], ident[:])
        nc.scalar.copy(bias[:], bias_ps[:, 0:8])

        xb = [[held("xb%d%d" % (c, u), [P, 2, HALF], F32) for u in range(2)] for c in range(2)]
        xp = [[held("xp%d%d" % (c, u), [P, HALF, 2], F32) for u in range(2)] for c in range(2)]
        for c in range(2):
            for t in range(4):
                bank = acc.tile([P, HALF], F32, name="bank")
                for a in range(PB):
                    w0 = (a * 4 + t) * 64
                    s0 = (a * 4 + t) * 32
                    nc.tensor.matmul_mx(bank[:], lhsT=w3p[:, w0: w0 + 64].bitcast(FP4X4),
                                        lhsT_scale=w3s[:, s0: s0 + 32].bitcast(U8),
                                        rhs=xs[c][:, a, :].bitcast(FP8X4),
                                        rhs_scale=xss[c][:, a, :].bitcast(U8),
                                        start=(a == 0), stop=(a == PB - 1))
                nc.scalar.activation(xb[c][t // 2][:, t % 2, :], bank[:], ACT.Identity, bias=bias[:, t: t + 1])
                if t % 2 == 1:
                    nc.scalar.copy(xp[c][t // 2][:], xb[c][t // 2][:].rearrange("p e j -> p j e"))

        vs = keep.tile([P, S], U8, name="vs", tag="xss_then_vs", align_bytes=64)
        nc.vector.tensor_copy(vs[:], tabs[:].bitcast(U8).indirect(offsets[:]))
        v0 = keep.tile([P, S], U32, name="v0", tag="tabs_then_v0", align_bytes=64)
        nc.vector.tensor_copy(v0[:], tab[0][:].bitcast(U32).indirect(offsets[:]))
        w2s = held("w2s", [P, H // 4], I32)
        nc.vector.tensor_copy(w2s[:].rearrange("p (t g w) -> p t g w", t=4, w=2),
                              w2s_raw[:].rearrange("p (g t w) -> p t g w", t=4, w=2))
        v1 = [held("v1%d" % c, [P, HALF], U32) for c in range(2)]
        nc.vector.tensor_copy(v1[0][:], tab[1][:].bitcast(U32).indirect(offsets[:, 0:32]))
        w2p = keep.tile([P, PA * H], I32, name="w2p", tag="tab0", align_bytes=64)
        nc.vector.tensor_copy(w2p[:].rearrange("p (a t g w) -> p a t g w", a=PA, t=4, w=8),
                              w2_raw[:].rearrange("p a (g t w) -> p a t g w", t=4, w=8))
        nc.vector.tensor_copy(v1[1][:], tab[1][:].bitcast(U32).indirect(offsets[:, 32:64]))

        def table_product(q, u, codes, scales):
            bank = acc.tile([P, 2, QUART], F32, name="bank")
            j0 = q * QUART
            for e in range(2):
                for a in range(PA):
                    moving = v0[:, j0: j0 + QUART] if a == 0 else v1[q // 2][:, j0 % HALF: j0 % HALF + QUART]
                    nc.tensor.matmul_mx(bank[:, e, :], lhsT=codes(a, u, e).bitcast(FP8X4),
                                        lhsT_scale=scales(a, u, e), rhs=moving.bitcast(FP8X4),
                                        rhs_scale=vs[ROW0 + 4 * a: P, j0: j0 + QUART],
                                        start=(a == 0), stop=(a == PA - 1))
            return bank[:].rearrange("p e j -> p j e")

        def x_pair(q, u):
            j0 = (q % 2) * QUART
            return xp[q // 2][u][:, j0: j0 + QUART, :]

        def w2_codes(a, u, e):
            c0 = (a * 4 + 2 * u + e) * P
            return w2p[:, c0: c0 + P]

        def w2_plane(a, u, e):
            c0 = (2 * u + e) * 32
            return w2s[ROW0 + 4 * a: P, c0: c0 + 32].bitcast(U8)

        w1b = [[held("w1b%d%d" % (a, u), [P, 4 * QUART], BF16) for u in range(2)] for a in range(PA)]
        w1c = [[held("w1c%d%d" % (a, u), [P, QUART], U32) for u in range(2)] for a in range(PA)]
        w1s = [[held("w1s%d%d" % (a, u), [P, QUART], U8) for u in range(2)] for a in range(PA)]

        def round_w1(a, u):
            src = w1_raw[a][:].rearrange("p i (g t h w) -> p t g h i w", t=4, h=2, w=4)
            dst = w1b[a][u][:].rearrange("p (e g h w i) -> p e g h i w", e=2, h=2, w=4, i=4)
            for e in range(2):
                nc.scalar.copy(dst[:, e], src[:, 2 * u + e])

        def quantise_w1(a, u):
            nc.vector.quantize_mx(w1c[a][u][:].bitcast(FP8X4), w1s[a][u][:], w1b[a][u][:])

        floor = [held("floor%d" % q, [P, 2, QUART, 2], F32) for q in range(NQ)]
        w1_pieces = [(a, u) for a in range(PA) for u in range(2)]
        for a, u in w1_pieces:
            round_w1(a, u)
        for q in range(NQ):
            for u in range(2):
                lo = table_product(q, u, w2_codes, w2_plane)
                nc.vector.tensor_tensor(floor[q][:, u], lo, x_pair(q, u), ALU.max)
            if q >= 1:
                quantise_w1(*w1_pieces[q - 1])
        quantise_w1(*w1_pieces[NQ - 1])

        w4b = held("w4b", [P, N, 4], BF16)
        nc.scalar.copy(w4b[:].rearrange("p (m w) t -> p m t w", w=4), w4_raw[:].rearrange("p t (m w) -> p m t w", w=4))
        w4c = held("w4c", [P, N], U32)
        w4s = held("w4s", [P, N], U8)
        w4_flat = w4b[:].rearrange("p n t -> p (n t)")

        def w1_codes(a, u, e):
            return w1c[a][u][:, e * P: (e + 1) * P]

        def w1_plane(a, u, e):
            return w1s[a][u][:, e * P: (e + 1) * P]

        ceil = {}
        hb = {}

        def upper(q, u):
            if u == 0:
                ceil[q] = ring.tile([P, 2, QUART, 2], F32, name="ceil")
            hi = table_product(q, u, w1_codes, w1_plane)
            nc.vector.tensor_tensor(ceil[q][:, u], hi, x_pair(q, u), ALU.min)

        def difference(q, j0, n):
            hb[q, j0] = ring.tile([P, n, 2, 2], BF16, name="hb", align_bytes=64)
            nc.vector.tensor_tensor(hb[q, j0][:], ceil[q][:, :, j0: j0 + n].rearrange("p u j e -> p j u e"),
                                    floor[q][:, :, j0: j0 + n].rearrange("p u j e -> p j u e"), ALU.subtract)

        out_v = out.rearrange("(c p) j -> p c j", p=P)

        def scores(q, j0, n):
            hc = ring.tile([P, n], U32, name="hc", align_bytes=64)
            hs = ring.tile([P, n], U8, name="hs", align_bytes=64)
            nc.vector.quantize_mx(hc[:].bitcast(FP8X4), hs[:], hb[q, j0][:].rearrange("p j u e -> p (j u e)"))
            res = ring.tile([P, NT, n], F32, name="res")
            for c in range(NT):
                y = ysum.tile([P, n], F32, name="y")
                nc.tensor.matmul_mx(y[:], lhsT=w4c[:, c * P: (c + 1) * P].bitcast(FP8X4),
                                    lhsT_scale=w4s[:, c * P: (c + 1) * P], rhs=hc[:].bitcast(FP8X4),
                                    rhs_scale=hs[:], start=True, stop=True)
                nc.scalar.activation(res[:, c, :], y[:], ACT.Sigmoid, bias=bias[:, 4 + c: 5 + c])
            col = q * QUART + j0
            queue = nc.scalar if col + n == S else nc.sync
            queue.dma_start(out_v[:, :, col: col + n], res[:])

        upper(0, 0)
        upper(1, 0)
        upper(0, 1)
        upper(1, 1)
        difference(0, 0, QUART)
        nc.vector.quantize_mx(w4c[:, 0:256].bitcast(FP8X4), w4s[:, 0:256], w4_flat[:, 0:1024])
        nc.vector.quantize_mx(w4c[:, 256:N].bitcast(FP8X4), w4s[:, 256:N], w4_flat[:, 1024:4 * N])
        scores(0, 0, QUART)
        difference(1, 0, QUART)
        upper(2, 0)
        upper(2, 1)
        scores(1, 0, QUART)
        difference(2, 0, P)
        upper(3, 0)
        scores(2, 0, P)
        difference(2, P, P)
        upper(3, 1)
        scores(2, P, P)
        difference(3, 0, P)
        difference(3, P, P)
        scores(3, 0, P)
        scores(3, P, P)
